import numpy as np
import ml_dtypes


def mxq(x, axis, fmt="e4m3"):
    dtype, down = {"e4m3": (ml_dtypes.float8_e4m3fn, 7), "e5m2": (ml_dtypes.float8_e5m2, 14)}[fmt]
    v = np.moveaxis(np.asarray(x, np.float32).astype(ml_dtypes.bfloat16).astype(np.float64), axis, -1)
    blocks = v.reshape(v.shape[:-1] + (-1, 32))
    amax = np.abs(blocks).max(-1, keepdims=True)
    byte = np.maximum(np.where(amax > 0, np.frexp(amax)[1] - 1 + 127, 0) - down, 1)
    scale = np.exp2(byte - 127.0)
    codes = (blocks / scale).astype(np.float32).astype(dtype).astype(np.float64)
    return np.moveaxis((codes * scale).reshape(v.shape), -1, axis)


WIDE = False


def mx_kscale(k):
    if not WIDE:
        return np.ones(k)
    levels = np.array([10, -10, 5, -5, 0])
    if k % 512:
        return np.exp2(np.random.permutation(np.resize(levels, k // 32))).repeat(32)
    a = np.empty((k // 512, 16))
    for p in range(k // 512):
        a[p, :8] = np.random.permutation(np.resize(levels, 8))
        for g in range(8):
            far = levels[np.abs(levels - a[p, g]) >= 10]
            a[p, g + 8] = far[np.random.randint(len(far))]
    return np.exp2(a.ravel()).repeat(32)


def f64(x):
    return np.asarray(x).astype(np.float64)


def striped(idx):
    return np.tile(np.asarray(idx).reshape(-1, 16).T, (8, 1)).astype(np.uint16)


def unstriped(offs):
    return offs[:16].T.reshape(-1).astype(np.int64)


E2M1 = np.array([0.0, 0.5, 1.0, 1.5, 2.0, 3.0, 4.0, 6.0, -0.0, -0.5, -1.0, -1.5, -2.0, -3.0, -4.0, -6.0])


def pack_weight(w, fmt):
    k, n = w.shape
    w = f64(np.asarray(w, np.float32).astype(ml_dtypes.bfloat16)).reshape(k // 32, 32, n)
    amax = np.abs(w).max(1)
    if fmt == "e4m3":
        byte = np.frexp(amax)[1] - 1 + 127 - 7
    else:
        mant, ex = np.frexp(amax / 6.0)
        byte = np.where(mant > 0.5, ex, ex - 1) + 127
    byte = np.clip(np.where(amax > 0, byte, 1), 1, 254)
    scaled = (w * np.exp2(127.0 - byte)[:, None, :]).reshape(k, n).astype(np.float32)
    by_word = np.ascontiguousarray(scaled.reshape(k // 512, 128, 4, n).transpose(0, 1, 3, 2))
    if fmt == "e4m3":
        words = by_word.astype(ml_dtypes.float8_e4m3fn).view(np.uint8)
    else:
        c = by_word.astype(ml_dtypes.float4_e2m1fn).view(np.uint8) & 0xF
        words = (c[..., 0::2] | (c[..., 1::2] << 4)).reshape(k // 512, 128, 2 * n)
    return np.ascontiguousarray(words), np.ascontiguousarray(byte.astype(np.uint8).reshape(k // 512, 16, n))


def unpack_weight(words, scales, fmt):
    g, _, n = scales.shape
    words = np.ascontiguousarray(words).reshape(g, 128, n, -1)
    if fmt == "e4m3":
        vals = words.view(ml_dtypes.float8_e4m3fn).astype(np.float64)
    else:
        nib = np.empty((g, 128, n, 4), np.uint8)
        nib[..., 0::2] = words & 0xF
        nib[..., 1::2] = words >> 4
        vals = E2M1[nib]
    vals = vals * np.repeat(np.exp2(scales.astype(np.float64) - 127.0), 8, axis=1)[..., None]
    return vals.transpose(0, 1, 3, 2).reshape(g * 512, n)


K, T, J, R, N = 512, 2048, 512, 512, 512


def setup_inputs():
    n = np.random.standard_normal
    idx = np.random.permutation(T)[:J]
    fk = mx_kscale(K)
    fr = mx_kscale(R)
    xtp = pack_weight(n((K, T)) / fk[:, None], "e4m3")
    wap = pack_weight(n((K, R)) * 1 / np.sqrt(K) * fk[:, None] * fr, "e2m1")
    wbp = pack_weight(n((R, N)) * 1 / np.sqrt(R) / fr[:, None], "e4m3")
    return {
        "xt_words": xtp[0],
        "xt_scales": xtp[1],
        "wa_words": wap[0],
        "wa_scales": wap[1],
        "dc": (np.random.uniform(0.3, 0.9, (R, 1))).astype(np.float32),
        "wb_words": wbp[0],
        "wb_scales": wbp[1],
        "rw": (np.random.uniform(0.5, 2.0, (1, J))).astype(np.float32),
        "offs": striped(idx),
    }


def reference(xt_words, xt_scales, wa_words, wa_scales, dc, wb_words, wb_scales, rw, offs):
    idx = unstriped(offs)
    xtu = unpack_weight(xt_words, xt_scales, "e4m3")
    wau = unpack_weight(wa_words, wa_scales, "e2m1")
    wbu = unpack_weight(wb_words, wb_scales, "e4m3")
    xtidxg = xtu[:, idx]
    a = wau.T @ xtidxg
    h1 = np.maximum(a, 0.0)
    hp = np.pad(h1, ((0, 0), (1, 0)))[:, :J]
    hid = h1 + f64(dc) * hp
    hidq = mxq(hid, 0, "e4m3")
    p = wbu.T @ hidq
    y = p * f64(rw)
    return y

@@ -1,0 +1,173 @@
+from contextlib import ExitStack
+
+import concourse.mybir as mybir
+from concourse.masks import make_identity
+
+K, T, J, R, N = 512, 2048, 512, 512, 512
+FLOPS = 2 * K * R * J + 2 * R * N * J
+
+F32 = mybir.dt.float32
+BF16 = mybir.dt.bfloat16
+I32 = mybir.dt.int32
+U32 = mybir.dt.uint32
+U16 = mybir.dt.uint16
+U8 = mybir.dt.uint8
+FP8X4 = mybir.dt.float8_e4m3fn_x4
+FP4X4 = mybir.dt.float4_e2m1fn_x4
+ALU = mybir.AluOpType
+ACT = mybir.ActivationFunctionType
+
+P = 128
+PACK = 4
+CH = 128
+NCH = J // CH
+HALF = J // 2
+
+
+def tile_list_hidden_with_previous_kernel(
+    tc, xt_words, xt_scales, wa_words, wa_scales, dc, wb_words, wb_scales, rw, offs, out
+):
+    nc = tc.nc
+    with ExitStack() as ctx:
+        sb = ctx.enter_context(tc.tile_pool(name="sb", bufs=1))
+        ps = ctx.enter_context(tc.psum_pool(name="ps", bufs=1))
+
+        offsets = sb.tile([P, J // 16], U16, name="offsets")
+        xt = sb.tile([P, T], I32, name="xt", align_bytes=64)
+        xs = sb.tile([P, T], U8, name="xs", align_bytes=64)
+        w_words = sb.tile([P, N], I32, name="w_words", align_bytes=64)
+        w_scales = sb.tile([P, N], U8, name="w_scales", align_bytes=64)
+        wa_dealt = sb.tile([P, 2 * R], U8, name="wa_dealt", align_bytes=64)
+        was_dealt = sb.tile([P, R], U8, name="was_dealt", align_bytes=64)
+        dc_t = sb.tile([P, PACK], F32, name="dc_t")
+        rw_t = sb.tile([P, PACK], F32, name="rw_t")
+        ident = sb.tile([P, P], F32, name="ident")
+        rw_all = sb.tile([P, J], F32, name="rw_all")
+        prev = sb.tile([P, PACK, J + 4], F32, name="prev")
+        xs_g = sb.tile([P, J], U8, name="xs_g", align_bytes=64)
+        xt_g = [sb.tile([P, HALF], U32, name=f"xt_g{h}", align_bytes=64) for h in range(2)]
+
+        nc.vector.memset(xs[:].bitcast(I32), 0)
+        nc.gpsimd.memset(w_scales[:].bitcast(I32), 0)
+        nc.vector.memset(prev[:, :, 0:1], 0.0)
+
+        nc.sync.dma_start(offsets[:], offs)
+        nc.sync.dma_start(w_words[:, 0 : R // 2], wa_words[0].bitcast(I32))
+        nc.sync.dma_start(xt[:], xt_words[0].rearrange("p n t -> p (n t)").bitcast(I32))
+        nc.scalar.dma_start(dc_t[:], dc.rearrange("(p t) o -> p (t o)", t=PACK))
+        for q in range(4):
+            nc.scalar.dma_start(xs[32 * q : 32 * q + 4, :].bitcast(I32), xt_scales[0, 4 * q : 4 * q + 4, :].bitcast(I32))
+        for q in range(4):
+            queue = nc.scalar if q < 3 else nc.gpsimd
+            queue.dma_start(w_scales[32 * q : 32 * q + 4, :].bitcast(I32), wa_scales[0, 4 * q : 4 * q + 4, :].bitcast(I32))
+        nc.gpsimd.dma_start(rw_t[:], rw[0].rearrange("(p c) -> p c", c=PACK))
+        make_identity(nc, ident[:])
+
+        nc.vector.tensor_copy(
+            wa_dealt[:].bitcast(U16).rearrange("p (t q) -> p t q", t=PACK),
+            w_words[:, 0 : R // 2].bitcast(U16).rearrange("p (q t) -> p t q", t=PACK),
+        )
+        nc.vector.tensor_copy(xs_g[:], xs[:].indirect(offsets[:]))
+        nc.vector.tensor_copy(
+            was_dealt[:].rearrange("p (t q) -> p t q", t=PACK),
+            w_scales[:].rearrange("p (q t) -> p t q", t=PACK),
+        )
+        nc.sync.dma_start(w_words[:], wb_words[0].rearrange("p n t -> p (n t)").bitcast(I32))
+        for q in range(4):
+            nc.sync.dma_start(w_scales[32 * q : 32 * q + 4, :].bitcast(I32), wb_scales[0, 4 * q : 4 * q + 4, :].bitcast(I32))
+
+        rw_ps = ps.tile([P, PACK, CH], F32, name="rw_ps", tag="b3")
+        for c in range(PACK):
+            nc.tensor.transpose(rw_ps[:, c, :], rw_t[:, c : c + 1].to_broadcast([P, P]), ident[:])
+        nc.scalar.activation(
+            rw_all[:].rearrange("p (n c) -> p n c", c=PACK), rw_ps[:].rearrange("p c n -> p n c"), ACT.Copy
+        )
+
+        for h in range(2):
+            nc.vector.tensor_copy(xt_g[h][:], xt[:].bitcast(U32).indirect(offsets[:, 16 * h : 16 * h + 16]))
+
+        a_ps = [ps.tile([P, PACK, CH], F32, name=f"a_ps{c}", tag=f"a{c}") for c in range(NCH)]
+        for c in range(NCH):
+            for t in range(PACK):
+                nc.tensor.matmul_mx(
+                    out=a_ps[c][:, t, :],
+                    lhsT=wa_dealt[:, 2 * P * t : 2 * P * (t + 1)].bitcast(FP4X4),
+                    lhsT_scale=was_dealt[:, P * t : P * (t + 1)],
+                    rhs=xt_g[c // 2][:, CH * (c % 2) : CH * (c % 2 + 1)].bitcast(FP8X4),
+                    rhs_scale=xs_g[:, CH * c : CH * (c + 1)],
+                    start=True,
+                    stop=True,
+                )
+
+        out_v = out.rearrange("(b p) j -> p b j", p=P)
+
+        def carry(c):
+            width = CH if c < NCH - 1 else CH - 1
+            lo = CH * c + 1
+            if c == 0:
+                nc.vector.scalar_tensor_tensor(
+                    prev[:, :, lo : lo + width],
+                    a_ps[c][:],
+                    0.0,
+                    dc_t[:].unsqueeze(2).to_broadcast([P, PACK, CH]),
+                    ALU.max,
+                    ALU.mult,
+                )
+            else:
+                h1 = sb.tile([P, PACK, CH], F32, name=f"h1_{c}")
+                nc.scalar.activation(h1[:, :, 0:width], a_ps[c][:, :, 0:width], ACT.Relu)
+                for t in range(PACK):
+                    nc.scalar.activation(
+                        prev[:, t, lo : lo + width], h1[:, t, 0:width], ACT.Copy, scale=dc_t[:, t : t + 1]
+                    )
+
+        hid = [sb.tile([P, CH, PACK], BF16, name=f"hid{c}", align_bytes=64) for c in range(NCH)]
+        codes = [sb.tile([P, CH], U32, name=f"codes{c}", align_bytes=64) for c in range(NCH)]
+        scales = [sb.tile([P, CH], U8, name=f"scales{c}", align_bytes=64) for c in range(NCH)]
+        p_ps = {}
+
+        def combine(c):
+            nc.vector.scalar_tensor_tensor(
+                hid[c][:],
+                a_ps[c][:].rearrange("p t j -> p j t"),
+                0.0,
+                prev[:, :, CH * c : CH * (c + 1)].rearrange("p t j -> p j t"),
+                ALU.max,
+                ALU.add,
+            )
+
+        def second(c):
+            nc.vector.quantize_mx(
+                out=codes[c][:].bitcast(FP8X4), scales=scales[c][:], in_=hid[c][:].rearrange("p j t -> p (j t)")
+            )
+            p_ps[c] = ps.tile([P, PACK, CH], F32, name=f"p_ps{c}", tag=f"b{c}")
+            for b in range(PACK):
+                nc.tensor.matmul_mx(
+                    out=p_ps[c][:, b, :],
+                    lhsT=w_words[:, P * b : P * (b + 1)].bitcast(FP8X4),
+                    lhsT_scale=w_scales[:, P * b : P * (b + 1)],
+                    rhs=codes[c][:].bitcast(FP8X4),
+                    rhs_scale=scales[c][:],
+                    start=True,
+                    stop=True,
+                )
+
+        def finish(c):
+            y = sb.tile([P, PACK, CH], F32, name=f"y{c}")
+            nc.vector.tensor_tensor(
+                y[:],
+                p_ps[c][:],
+                rw_all[:, CH * c : CH * (c + 1)].unsqueeze(1).to_broadcast([P, PACK, CH]),
+                ALU.mult,
+            )
+            nc.sync.dma_start(out_v[:, :, CH * c : CH * (c + 1)], y[:])
+
+        for c in range(NCH):
+            carry(c)
+        for c in range(NCH + 1):
+            if c < NCH:
+                combine(c)
+            if c > 0:
+                finish(c - 1)
+            if c < NCH:
+                second(c)

@@ -30,59 +30,70 @@ def tile_list_hidden_with_previous_kernel(
     nc = tc.nc
     with ExitStack() as ctx:
         sb = ctx.enter_context(tc.tile_pool(name="sb", bufs=1))
+        late = ctx.enter_context(tc.tile_pool(name="late", bufs=1))
         ps = ctx.enter_context(tc.psum_pool(name="ps", bufs=1))
 
         offsets = sb.tile([P, J // 16], U16, name="offsets")
-        xt = sb.tile([P, T], I32, name="xt", align_bytes=64)
+        zeros = sb.tile([P, PACK], F32, name="zeros", tag="xt", align_bytes=64)
         xs = sb.tile([P, T], U8, name="xs", align_bytes=64)
-        w_words = sb.tile([P, N], I32, name="w_words", align_bytes=64)
-        w_scales = sb.tile([P, N], U8, name="w_scales", align_bytes=64)
+        wa_raw = late.tile([P, 2 * R], U8, name="wa_raw", offset=0, align_bytes=64)
+        w_scales = sb.tile([P, R], U8, name="w_scales", tag="second_half", align_bytes=64)
         wa_dealt = sb.tile([P, 2 * R], U8, name="wa_dealt", align_bytes=64)
         was_dealt = sb.tile([P, R], U8, name="was_dealt", align_bytes=64)
-        dc_t = sb.tile([P, PACK], F32, name="dc_t")
         rw_t = sb.tile([P, PACK], F32, name="rw_t")
         ident = sb.tile([P, P], F32, name="ident")
         rw_all = sb.tile([P, J], F32, name="rw_all")
-        prev = sb.tile([P, PACK, J + 4], F32, name="prev")
+        prev01 = sb.tile([P, PACK, 2 * CH + 4], F32, name="prev01")
+        prev = [prev01[:, :, 0 : CH + 1], prev01[:, :, CH : 2 * CH + 1]] + [
+            sb.tile([P, PACK, CH + 4], F32, name=f"prev{c}")[:, :, 0 : CH + 1] for c in range(2, NCH)
+        ]
         xs_g = sb.tile([P, J], U8, name="xs_g", align_bytes=64)
-        xt_g = [sb.tile([P, HALF], U32, name=f"xt_g{h}", align_bytes=64) for h in range(2)]
 
+        nc.gpsimd.memset(zeros[:], 0.0)
         nc.vector.memset(xs[:].bitcast(I32), 0)
-        nc.gpsimd.memset(w_scales[:].bitcast(I32), 0)
-        nc.vector.memset(prev[:, :, 0:1], 0.0)
+        nc.vector.tensor_copy(prev[0][:, :, 0], zeros[:])
+        nc.vector.memset(w_scales[:].bitcast(I32), 0)
+        xt = sb.tile([P, T], I32, name="xt", tag="xt", align_bytes=64)
 
         nc.sync.dma_start(offsets[:], offs)
-        nc.sync.dma_start(w_words[:, 0 : R // 2], wa_words[0].bitcast(I32))
+        with nc.allow_non_contiguous_dma(reason="one weight a partition for each chunk"):
+            nc.scalar.dma_start(rw_t[:], rw[0].rearrange("(c p) -> p c", p=P))
+        nc.sync.dma_start(wa_raw[:].bitcast(I32), wa_words[0].bitcast(I32))
+        for q in range(4):
+            queue = nc.sync if q < 2 else nc.scalar
+            queue.dma_start(xs[32 * q : 32 * q + 4, :].bitcast(I32), xt_scales[0, 4 * q : 4 * q + 4, :].bitcast(I32))
         nc.sync.dma_start(xt[:], xt_words[0].rearrange("p n t -> p (n t)").bitcast(I32))
-        nc.scalar.dma_start(dc_t[:], dc.rearrange("(p t) o -> p (t o)", t=PACK))
         for q in range(4):
-            nc.scalar.dma_start(xs[32 * q : 32 * q + 4, :].bitcast(I32), xt_scales[0, 4 * q : 4 * q + 4, :].bitcast(I32))
-        for q in range(4):
-            queue = nc.scalar if q < 3 else nc.gpsimd
-            queue.dma_start(w_scales[32 * q : 32 * q + 4, :].bitcast(I32), wa_scales[0, 4 * q : 4 * q + 4, :].bitcast(I32))
-        nc.gpsimd.dma_start(rw_t[:], rw[0].rearrange("(p c) -> p c", c=PACK))
+            nc.sync.dma_start(w_scales[32 * q : 32 * q + 4, :].bitcast(I32), wa_scales[0, 4 * q : 4 * q + 4, :].bitcast(I32))
         make_identity(nc, ident[:])
 
         nc.vector.tensor_copy(
             wa_dealt[:].bitcast(U16).rearrange("p (t q) -> p t q", t=PACK),
-            w_words[:, 0 : R // 2].bitcast(U16).rearrange("p (q t) -> p t q", t=PACK),
+            wa_raw[:].bitcast(U16).rearrange("p (q t) -> p t q", t=PACK),
         )
         nc.vector.tensor_copy(xs_g[:], xs[:].indirect(offsets[:]))
         nc.vector.tensor_copy(
             was_dealt[:].rearrange("p (t q) -> p t q", t=PACK),
             w_scales[:].rearrange("p (q t) -> p t q", t=PACK),
         )
-        nc.sync.dma_start(w_words[:], wb_words[0].rearrange("p n t -> p (n t)").bitcast(I32))
+        dc_t = late.tile([P, PACK], F32, name="dc_t", offset=0, align_bytes=64)
+        wb_scale = late.tile([P, N], U8, name="wb_scale", offset=64, align_bytes=64)
+        wb_word = late.tile([P, 4 * N], U8, name="wb_word", offset=64 + N, align_bytes=64)
+        nc.gpsimd.memset(wb_scale[:].bitcast(I32), 0)
+        nc.sync.dma_start(dc_t[:], dc.rearrange("(p t) o -> p (t o)", t=PACK))
+        nc.sync.dma_start(wb_word[:].bitcast(I32), wb_words[0].rearrange("p n t -> p (n t)").bitcast(I32))
         for q in range(4):
-            nc.sync.dma_start(w_scales[32 * q : 32 * q + 4, :].bitcast(I32), wb_scales[0, 4 * q : 4 * q + 4, :].bitcast(I32))
+            nc.sync.dma_start(wb_scale[32 * q : 32 * q + 4, :].bitcast(I32), wb_scales[0, 4 * q : 4 * q + 4, :].bitcast(I32))
 
-        rw_ps = ps.tile([P, PACK, CH], F32, name="rw_ps", tag="b3")
-        for c in range(PACK):
-            nc.tensor.transpose(rw_ps[:, c, :], rw_t[:, c : c + 1].to_broadcast([P, P]), ident[:])
-        nc.scalar.activation(
-            rw_all[:].rearrange("p (n c) -> p n c", c=PACK), rw_ps[:].rearrange("p c n -> p n c"), ACT.Copy
-        )
+        for c in range(NCH):
+            rw_ps = ps.tile([P, PACK, CH], F32, name=f"rw_ps{c}", tag=f"a{c}")
+            nc.tensor.transpose(rw_ps[:, 0, :], rw_t[:, c : c + 1].to_broadcast([P, P]), ident[:])
+            nc.scalar.activation(rw_all[:, CH * c : CH * (c + 1)], rw_ps[:, 0, :], ACT.Copy)
 
+        xt_g = [
+            sb.tile([P, HALF], U32, name="xt_g0", align_bytes=64),
+            sb.tile([P, HALF], U32, name="xt_g1", tag="second_half", align_bytes=64),
+        ]
         for h in range(2):
             nc.vector.tensor_copy(xt_g[h][:], xt[:].bitcast(U32).indirect(offsets[:, 16 * h : 16 * h + 16]))
 
@@ -103,10 +114,9 @@ def tile_list_hidden_with_previous_kernel(
 
         def carry(c):
             width = CH if c < NCH - 1 else CH - 1
-            lo = CH * c + 1
-            if c == 0:
+            if c < 2:
                 nc.vector.scalar_tensor_tensor(
-                    prev[:, :, lo : lo + width],
+                    prev[c][:, :, 1 : 1 + width],
                     a_ps[c][:],
                     0.0,
                     dc_t[:].unsqueeze(2).to_broadcast([P, PACK, CH]),
@@ -116,9 +126,10 @@ def tile_list_hidden_with_previous_kernel(
             else:
                 h1 = sb.tile([P, PACK, CH], F32, name=f"h1_{c}")
                 nc.scalar.activation(h1[:, :, 0:width], a_ps[c][:, :, 0:width], ACT.Relu)
+                nc.scalar.activation(prev[c][:, :, 0:1], prev[c - 1][:, :, CH : CH + 1], ACT.Copy)
                 for t in range(PACK):
                     nc.scalar.activation(
-                        prev[:, t, lo : lo + width], h1[:, t, 0:width], ACT.Copy, scale=dc_t[:, t : t + 1]
+                        prev[c][:, t, 1 : 1 + width], h1[:, t, 0:width], ACT.Copy, scale=dc_t[:, t : t + 1]
                     )
 
         hid = [sb.tile([P, CH, PACK], BF16, name=f"hid{c}", align_bytes=64) for c in range(NCH)]
@@ -131,7 +142,7 @@ def tile_list_hidden_with_previous_kernel(
                 hid[c][:],
                 a_ps[c][:].rearrange("p t j -> p j t"),
                 0.0,
-                prev[:, :, CH * c : CH * (c + 1)].rearrange("p t j -> p j t"),
+                prev[c][:, :, 0:CH].rearrange("p t j -> p j t"),
                 ALU.max,
                 ALU.add,
             )
@@ -144,8 +155,8 @@ def tile_list_hidden_with_previous_kernel(
             for b in range(PACK):
                 nc.tensor.matmul_mx(
                     out=p_ps[c][:, b, :],
-                    lhsT=w_words[:, P * b : P * (b + 1)].bitcast(FP8X4),
-                    lhsT_scale=w_scales[:, P * b : P * (b + 1)],
+                    lhsT=wb_word[:, 4 * P * b : 4 * P * (b + 1)].bitcast(FP8X4),
+                    lhsT_scale=wb_scale[:, P * b : P * (b + 1)],
                     rhs=codes[c][:].bitcast(FP8X4),
                     rhs_scale=scales[c][:],
                     start=True,
@@ -164,10 +175,15 @@ def tile_list_hidden_with_previous_kernel(
 
         for c in range(NCH):
             carry(c)
-        for c in range(NCH + 1):
-            if c < NCH:
-                combine(c)
-            if c > 0:
-                finish(c - 1)
-            if c < NCH:
-                second(c)
+        combine(0)
+        combine(1)
+        second(0)
+        second(1)
+        combine(2)
+        second(2)
+        finish(0)
+        combine(3)
+        second(3)
+        finish(1)
+        finish(2)
+        finish(3)

@@ -43,21 +43,20 @@ def tile_list_hidden_with_previous_kernel(
         rw_t = sb.tile([P, PACK], F32, name="rw_t")
         ident = sb.tile([P, P], F32, name="ident")
         rw_all = sb.tile([P, J], F32, name="rw_all")
-        prev01 = sb.tile([P, PACK, 2 * CH + 4], F32, name="prev01")
-        prev = [prev01[:, :, 0 : CH + 1], prev01[:, :, CH : 2 * CH + 1]] + [
-            sb.tile([P, PACK, CH + 4], F32, name=f"prev{c}")[:, :, 0 : CH + 1] for c in range(2, NCH)
-        ]
+        prev_woven = {c: sb.tile([P, CH + 1, PACK], F32, name=f"prev_woven{c}") for c in (0, 2)}
+        prev_planes = {c: sb.tile([P, PACK, CH + 4], F32, name=f"prev_planes{c}") for c in (1, 3)}
+        h1 = {c: sb.tile([P, PACK, CH], F32, name=f"h1_{c}") for c in (1, 3)}
+        rw_planes = sb.tile([P, PACK, P], F32, name="rw_planes")
         xs_g = sb.tile([P, J], U8, name="xs_g", align_bytes=64)
 
         nc.gpsimd.memset(zeros[:], 0.0)
         nc.vector.memset(xs[:].bitcast(I32), 0)
-        nc.vector.tensor_copy(prev[0][:, :, 0], zeros[:])
+        nc.vector.tensor_copy(prev_woven[0][:, 0, :], zeros[:])
         nc.vector.memset(w_scales[:].bitcast(I32), 0)
         xt = sb.tile([P, T], I32, name="xt", tag="xt", align_bytes=64)
 
         nc.sync.dma_start(offsets[:], offs)
-        with nc.allow_non_contiguous_dma(reason="one weight a partition for each chunk"):
-            nc.scalar.dma_start(rw_t[:], rw[0].rearrange("(c p) -> p c", p=P))
+        nc.scalar.dma_start(rw_t[:], rw[0].rearrange("(p c) -> p c", c=PACK))
         nc.sync.dma_start(wa_raw[:].bitcast(I32), wa_words[0].bitcast(I32))
         for q in range(4):
             queue = nc.sync if q < 2 else nc.scalar
@@ -88,7 +87,10 @@ def tile_list_hidden_with_previous_kernel(
         for c in range(NCH):
             rw_ps = ps.tile([P, PACK, CH], F32, name=f"rw_ps{c}", tag=f"a{c}")
             nc.tensor.transpose(rw_ps[:, 0, :], rw_t[:, c : c + 1].to_broadcast([P, P]), ident[:])
-            nc.scalar.activation(rw_all[:, CH * c : CH * (c + 1)], rw_ps[:, 0, :], ACT.Copy)
+            nc.scalar.activation(rw_planes[:, c, :], rw_ps[:, 0, :], ACT.Copy)
+        nc.scalar.activation(
+            rw_all[:].rearrange("p (n c) -> p n c", c=PACK), rw_planes[:].rearrange("p c n -> p n c"), ACT.Copy
+        )
 
         xt_g = [
             sb.tile([P, HALF], U32, name="xt_g0", align_bytes=64),
@@ -113,24 +115,25 @@ def tile_list_hidden_with_previous_kernel(
         out_v = out.rearrange("(b p) j -> p b j", p=P)
 
         def carry(c):
-            width = CH if c < NCH - 1 else CH - 1
-            if c < 2:
+            if c % 2 == 0:
                 nc.vector.scalar_tensor_tensor(
-                    prev[c][:, :, 1 : 1 + width],
-                    a_ps[c][:],
+                    prev_woven[c][:, 1 : CH + 1, :],
+                    a_ps[c][:].rearrange("p t j -> p j t"),
                     0.0,
-                    dc_t[:].unsqueeze(2).to_broadcast([P, PACK, CH]),
+                    dc_t[:].unsqueeze(1).to_broadcast([P, CH, PACK]),
                     ALU.max,
                     ALU.mult,
                 )
             else:
-                h1 = sb.tile([P, PACK, CH], F32, name=f"h1_{c}")
-                nc.scalar.activation(h1[:, :, 0:width], a_ps[c][:, :, 0:width], ACT.Relu)
-                nc.scalar.activation(prev[c][:, :, 0:1], prev[c - 1][:, :, CH : CH + 1], ACT.Copy)
+                width = CH if c < NCH - 1 else CH - 1
+                nc.scalar.activation(h1[c][:], a_ps[c][:], ACT.Relu)
+                nc.scalar.activation(prev_planes[c][:, :, 0], prev_woven[c - 1][:, CH, :], ACT.Copy)
                 for t in range(PACK):
                     nc.scalar.activation(
-                        prev[c][:, t, 1 : 1 + width], h1[:, t, 0:width], ACT.Copy, scale=dc_t[:, t : t + 1]
+                        prev_planes[c][:, t, 1 : 1 + width], h1[c][:, t, 0:width], ACT.Copy, scale=dc_t[:, t : t + 1]
                     )
+                if c < NCH - 1:
+                    nc.scalar.activation(prev_woven[c + 1][:, 0, :], prev_planes[c][:, :, CH], ACT.Copy)
 
         hid = [sb.tile([P, CH, PACK], BF16, name=f"hid{c}", align_bytes=64) for c in range(NCH)]
         codes = [sb.tile([P, CH], U32, name=f"codes{c}", align_bytes=64) for c in range(NCH)]
@@ -138,14 +141,22 @@ def tile_list_hidden_with_previous_kernel(
         p_ps = {}
 
         def combine(c):
-            nc.vector.scalar_tensor_tensor(
-                hid[c][:],
-                a_ps[c][:].rearrange("p t j -> p j t"),
-                0.0,
-                prev[c][:, :, 0:CH].rearrange("p t j -> p j t"),
-                ALU.max,
-                ALU.add,
-            )
+            if c % 2 == 0:
+                nc.vector.scalar_tensor_tensor(
+                    hid[c][:],
+                    a_ps[c][:].rearrange("p t j -> p j t"),
+                    0.0,
+                    prev_woven[c][:, 0:CH, :],
+                    ALU.max,
+                    ALU.add,
+                )
+            else:
+                nc.vector.tensor_tensor(
+                    hid[c][:].rearrange("p (g i) t -> p g t i", i=4),
+                    h1[c][:].rearrange("p t (g i) -> p g t i", i=4),
+                    prev_planes[c][:, :, 0:CH].rearrange("p t (g i) -> p g t i", i=4),
+                    ALU.add,
+                )
 
         def second(c):
             nc.vector.quantize_mx(
@@ -163,27 +174,30 @@ def tile_list_hidden_with_previous_kernel(
                     stop=True,
                 )
 
-        def finish(c):
-            y = sb.tile([P, PACK, CH], F32, name=f"y{c}")
+        def finish(c, lo, hi):
+            y = sb.tile([P, hi - lo, CH], F32, name=f"y{c}_{lo}")
             nc.vector.tensor_tensor(
                 y[:],
-                p_ps[c][:],
-                rw_all[:, CH * c : CH * (c + 1)].unsqueeze(1).to_broadcast([P, PACK, CH]),
+                p_ps[c][:, lo:hi, :],
+                rw_all[:, CH * c : CH * (c + 1)].unsqueeze(1).to_broadcast([P, hi - lo, CH]),
                 ALU.mult,
             )
-            nc.sync.dma_start(out_v[:, :, CH * c : CH * (c + 1)], y[:])
+            nc.sync.dma_start(out_v[:, lo:hi, CH * c : CH * (c + 1)], y[:])
 
-        for c in range(NCH):
-            carry(c)
+        carry(0)
+        carry(1)
         combine(0)
-        combine(1)
+        carry(2)
+        carry(3)
         second(0)
-        second(1)
+        combine(1)
         combine(2)
-        second(2)
-        finish(0)
+        second(1)
         combine(3)
+        second(2)
+        finish(0, 0, 4)
         second(3)
-        finish(1)
-        finish(2)
-        finish(3)
+        finish(1, 0, 4)
+        finish(2, 0, 4)
+        finish(3, 0, 2)
+        finish(3, 2, 4)

from contextlib import ExitStack

import concourse.mybir as mybir
from concourse.masks import make_identity

K, T, J, R, N = 512, 2048, 512, 512, 512
FLOPS = 2 * K * R * J + 2 * R * N * J

F32 = mybir.dt.float32
BF16 = mybir.dt.bfloat16
I32 = mybir.dt.int32
U32 = mybir.dt.uint32
U16 = mybir.dt.uint16
U8 = mybir.dt.uint8
FP8X4 = mybir.dt.float8_e4m3fn_x4
FP4X4 = mybir.dt.float4_e2m1fn_x4
ALU = mybir.AluOpType
ACT = mybir.ActivationFunctionType

P = 128
PACK = 4
CH = 128
NCH = J // CH
HALF = J // 2


def tile_list_hidden_with_previous_kernel(
    tc, xt_words, xt_scales, wa_words, wa_scales, dc, wb_words, wb_scales, rw, offs, out
):
    nc = tc.nc
    with ExitStack() as ctx:
        sb = ctx.enter_context(tc.tile_pool(name="sb", bufs=1))
        late = ctx.enter_context(tc.tile_pool(name="late", bufs=1))
        ps = ctx.enter_context(tc.psum_pool(name="ps", bufs=1))

        offsets = sb.tile([P, J // 16], U16, name="offsets")
        zeros = sb.tile([P, PACK], F32, name="zeros", tag="xt", align_bytes=64)
        xs = sb.tile([P, T], U8, name="xs", align_bytes=64)
        wa_raw = late.tile([P, 2 * R], U8, name="wa_raw", offset=0, align_bytes=64)
        w_scales = sb.tile([P, R], U8, name="w_scales", tag="second_half", align_bytes=64)
        wa_dealt = sb.tile([P, 2 * R], U8, name="wa_dealt", align_bytes=64)
        was_dealt = sb.tile([P, R], U8, name="was_dealt", align_bytes=64)
        rw_t = sb.tile([P, PACK], F32, name="rw_t")
        ident = sb.tile([P, P], F32, name="ident")
        rw_all = sb.tile([P, J], F32, name="rw_all")
        prev_woven = {c: sb.tile([P, CH + 1, PACK], F32, name=f"prev_woven{c}") for c in (0, 2)}
        prev_planes = {c: sb.tile([P, PACK, CH + 4], F32, name=f"prev_planes{c}") for c in (1, 3)}
        h1 = {c: sb.tile([P, PACK, CH], F32, name=f"h1_{c}") for c in (1, 3)}
        rw_planes = sb.tile([P, PACK, P], F32, name="rw_planes")
        xs_g = sb.tile([P, J], U8, name="xs_g", align_bytes=64)

        nc.gpsimd.memset(zeros[:], 0.0)
        nc.vector.memset(xs[:].bitcast(I32), 0)
        nc.vector.tensor_copy(prev_woven[0][:, 0, :], zeros[:])
        nc.vector.memset(w_scales[:].bitcast(I32), 0)
        xt = sb.tile([P, T], I32, name="xt", tag="xt", align_bytes=64)

        nc.sync.dma_start(offsets[:], offs)
        nc.scalar.dma_start(rw_t[:], rw[0].rearrange("(p c) -> p c", c=PACK))
        nc.sync.dma_start(wa_raw[:].bitcast(I32), wa_words[0].bitcast(I32))
        for q in range(4):
            queue = nc.sync if q < 2 else nc.scalar
            queue.dma_start(xs[32 * q : 32 * q + 4, :].bitcast(I32), xt_scales[0, 4 * q : 4 * q + 4, :].bitcast(I32))
        nc.sync.dma_start(xt[:], xt_words[0].rearrange("p n t -> p (n t)").bitcast(I32))
        for q in range(4):
            nc.sync.dma_start(w_scales[32 * q : 32 * q + 4, :].bitcast(I32), wa_scales[0, 4 * q : 4 * q + 4, :].bitcast(I32))
        make_identity(nc, ident[:])

        nc.vector.tensor_copy(
            wa_dealt[:].bitcast(U16).rearrange("p (t q) -> p t q", t=PACK),
            wa_raw[:].bitcast(U16).rearrange("p (q t) -> p t q", t=PACK),
        )
        nc.vector.tensor_copy(xs_g[:], xs[:].indirect(offsets[:]))
        nc.vector.tensor_copy(
            was_dealt[:].rearrange("p (t q) -> p t q", t=PACK),
            w_scales[:].rearrange("p (q t) -> p t q", t=PACK),
        )
        dc_t = late.tile([P, PACK], F32, name="dc_t", offset=0, align_bytes=64)
        wb_scale = late.tile([P, N], U8, name="wb_scale", offset=64, align_bytes=64)
        wb_word = late.tile([P, 4 * N], U8, name="wb_word", offset=64 + N, align_bytes=64)
        nc.gpsimd.memset(wb_scale[:].bitcast(I32), 0)
        nc.sync.dma_start(dc_t[:], dc.rearrange("(p t) o -> p (t o)", t=PACK))
        nc.sync.dma_start(wb_word[:].bitcast(I32), wb_words[0].rearrange("p n t -> p (n t)").bitcast(I32))
        for q in range(4):
            nc.sync.dma_start(wb_scale[32 * q : 32 * q + 4, :].bitcast(I32), wb_scales[0, 4 * q : 4 * q + 4, :].bitcast(I32))

        for c in range(NCH):
            rw_ps = ps.tile([P, PACK, CH], F32, name=f"rw_ps{c}", tag=f"a{c}")
            nc.tensor.transpose(rw_ps[:, 0, :], rw_t[:, c : c + 1].to_broadcast([P, P]), ident[:])
            nc.scalar.activation(rw_planes[:, c, :], rw_ps[:, 0, :], ACT.Copy)
        nc.scalar.activation(
            rw_all[:].rearrange("p (n c) -> p n c", c=PACK), rw_planes[:].rearrange("p c n -> p n c"), ACT.Copy
        )

        xt_g = [
            sb.tile([P, HALF], U32, name="xt_g0", align_bytes=64),
            sb.tile([P, HALF], U32, name="xt_g1", tag="second_half", align_bytes=64),
        ]
        for h in range(2):
            nc.vector.tensor_copy(xt_g[h][:], xt[:].bitcast(U32).indirect(offsets[:, 16 * h : 16 * h + 16]))

        a_ps = [ps.tile([P, PACK, CH], F32, name=f"a_ps{c}", tag=f"a{c}") for c in range(NCH)]
        for c in range(NCH):
            for t in range(PACK):
                nc.tensor.matmul_mx(
                    out=a_ps[c][:, t, :],
                    lhsT=wa_dealt[:, 2 * P * t : 2 * P * (t + 1)].bitcast(FP4X4),
                    lhsT_scale=was_dealt[:, P * t : P * (t + 1)],
                    rhs=xt_g[c // 2][:, CH * (c % 2) : CH * (c % 2 + 1)].bitcast(FP8X4),
                    rhs_scale=xs_g[:, CH * c : CH * (c + 1)],
                    start=True,
                    stop=True,
                )

        out_v = out.rearrange("(b p) j -> p b j", p=P)

        def carry(c):
            if c % 2 == 0:
                nc.vector.scalar_tensor_tensor(
                    prev_woven[c][:, 1 : CH + 1, :],
                    a_ps[c][:].rearrange("p t j -> p j t"),
                    0.0,
                    dc_t[:].unsqueeze(1).to_broadcast([P, CH, PACK]),
                    ALU.max,
                    ALU.mult,
                )
            else:
                width = CH if c < NCH - 1 else CH - 1
                nc.scalar.activation(h1[c][:], a_ps[c][:], ACT.Relu)
                nc.scalar.activation(prev_planes[c][:, :, 0], prev_woven[c - 1][:, CH, :], ACT.Copy)
                for t in range(PACK):
                    nc.scalar.activation(
                        prev_planes[c][:, t, 1 : 1 + width], h1[c][:, t, 0:width], ACT.Copy, scale=dc_t[:, t : t + 1]
                    )
                if c < NCH - 1:
                    nc.scalar.activation(prev_woven[c + 1][:, 0, :], prev_planes[c][:, :, CH], ACT.Copy)

        hid = [sb.tile([P, CH, PACK], BF16, name=f"hid{c}", align_bytes=64) for c in range(NCH)]
        codes = [sb.tile([P, CH], U32, name=f"codes{c}", align_bytes=64) for c in range(NCH)]
        scales = [sb.tile([P, CH], U8, name=f"scales{c}", align_bytes=64) for c in range(NCH)]
        p_ps = {}

        def combine(c):
            if c % 2 == 0:
                nc.vector.scalar_tensor_tensor(
                    hid[c][:],
                    a_ps[c][:].rearrange("p t j -> p j t"),
                    0.0,
                    prev_woven[c][:, 0:CH, :],
                    ALU.max,
                    ALU.add,
                )
            else:
                nc.vector.tensor_tensor(
                    hid[c][:].rearrange("p (g i) t -> p g t i", i=4),
                    h1[c][:].rearrange("p t (g i) -> p g t i", i=4),
                    prev_planes[c][:, :, 0:CH].rearrange("p t (g i) -> p g t i", i=4),
                    ALU.add,
                )

        def second(c):
            nc.vector.quantize_mx(
                out=codes[c][:].bitcast(FP8X4), scales=scales[c][:], in_=hid[c][:].rearrange("p j t -> p (j t)")
            )
            p_ps[c] = ps.tile([P, PACK, CH], F32, name=f"p_ps{c}", tag=f"b{c}")
            for b in range(PACK):
                nc.tensor.matmul_mx(
                    out=p_ps[c][:, b, :],
                    lhsT=wb_word[:, 4 * P * b : 4 * P * (b + 1)].bitcast(FP8X4),
                    lhsT_scale=wb_scale[:, P * b : P * (b + 1)],
                    rhs=codes[c][:].bitcast(FP8X4),
                    rhs_scale=scales[c][:],
                    start=True,
                    stop=True,
                )

        def finish(c, lo, hi):
            y = sb.tile([P, hi - lo, CH], F32, name=f"y{c}_{lo}")
            nc.vector.tensor_tensor(
                y[:],
                p_ps[c][:, lo:hi, :],
                rw_all[:, CH * c : CH * (c + 1)].unsqueeze(1).to_broadcast([P, hi - lo, CH]),
                ALU.mult,
            )
            nc.sync.dma_start(out_v[:, lo:hi, CH * c : CH * (c + 1)], y[:])

        carry(0)
        carry(1)
        combine(0)
        carry(2)
        carry(3)
        second(0)
        combine(1)
        combine(2)
        second(1)
        combine(3)
        second(2)
        finish(0, 0, 4)
        second(3)
        finish(1, 0, 4)
        finish(2, 0, 4)
        finish(3, 0, 2)
        finish(3, 2, 4)
